import numpy as np
import ml_dtypes


def mxq(x, axis, fmt="e4m3"):
    dtype, down = {"e4m3": (ml_dtypes.float8_e4m3fn, 7), "e5m2": (ml_dtypes.float8_e5m2, 14)}[fmt]
    v = np.moveaxis(np.asarray(x, np.float32).astype(ml_dtypes.bfloat16).astype(np.float64), axis, -1)
    blocks = v.reshape(v.shape[:-1] + (-1, 32))
    amax = np.abs(blocks).max(-1, keepdims=True)
    byte = np.maximum(np.where(amax > 0, np.frexp(amax)[1] - 1 + 127, 0) - down, 1)
    scale = np.exp2(byte - 127.0)
    codes = (blocks / scale).astype(np.float32).astype(dtype).astype(np.float64)
    return np.moveaxis((codes * scale).reshape(v.shape), -1, axis)


WIDE = False


def mx_kscale(k):
    if not WIDE:
        return np.ones(k)
    levels = np.array([10, -10, 5, -5, 0])
    if k % 512:
        return np.exp2(np.random.permutation(np.resize(levels, k // 32))).repeat(32)
    a = np.empty((k // 512, 16))
    for p in range(k // 512):
        a[p, :8] = np.random.permutation(np.resize(levels, 8))
        for g in range(8):
            far = levels[np.abs(levels - a[p, g]) >= 10]
            a[p, g + 8] = far[np.random.randint(len(far))]
    return np.exp2(a.ravel()).repeat(32)


BF16 = ml_dtypes.bfloat16


def bf(x):
    return np.asarray(x, np.float32).astype(BF16)


def f64(x):
    return np.asarray(x).astype(np.float64)


E2M1 = np.array([0.0, 0.5, 1.0, 1.5, 2.0, 3.0, 4.0, 6.0, -0.0, -0.5, -1.0, -1.5, -2.0, -3.0, -4.0, -6.0])


def pack_weight(w, fmt):
    k, n = w.shape
    w = f64(bf(w)).reshape(k // 32, 32, n)
    amax = np.abs(w).max(1)
    if fmt == "e4m3":
        byte = np.frexp(amax)[1] - 1 + 127 - 7
    else:
        mant, ex = np.frexp(amax / 6.0)
        byte = np.where(mant > 0.5, ex, ex - 1) + 127
    byte = np.clip(np.where(amax > 0, byte, 1), 1, 254)
    scaled = (w * np.exp2(127.0 - byte)[:, None, :]).reshape(k, n).astype(np.float32)
    by_word = np.ascontiguousarray(scaled.reshape(k // 512, 128, 4, n).transpose(0, 1, 3, 2))
    if fmt == "e4m3":
        words = by_word.astype(ml_dtypes.float8_e4m3fn).view(np.uint8)
    else:
        c = by_word.astype(ml_dtypes.float4_e2m1fn).view(np.uint8) & 0xF
        words = c[..., 0::2] | (c[..., 1::2] << 4)
    return np.ascontiguousarray(words), np.ascontiguousarray(byte.astype(np.uint8).reshape(k // 512, 16, n))


def unpack_weight(words, scales, fmt):
    g, p, n, _ = words.shape
    if fmt == "e4m3":
        vals = np.ascontiguousarray(words).view(ml_dtypes.float8_e4m3fn).astype(np.float64)
    else:
        nib = np.empty((g, p, n, 4), np.uint8)
        nib[..., 0::2] = words & 0xF
        nib[..., 1::2] = words >> 4
        vals = E2M1[nib]
    vals = vals * np.repeat(np.exp2(scales.astype(np.float64) - 127.0), 8, axis=1)[..., None]
    return vals.transpose(0, 1, 3, 2).reshape(g * 512, n)
def pack4(w):
    words, scales = pack_weight(w, "e2m1")
    return words.reshape(words.shape[0], 128, -1), scales


def unpack4(words, scales):
    return unpack_weight(words.reshape(words.shape[0], 128, -1, 2), scales, "e2m1")


D, S, T, C = 512, 2048, 2048, 640


def draw0():
    s, r = mx_kscale(D), mx_kscale(T)
    f1 = np.random.standard_normal((D, S)) * s[:, None]
    f2 = np.random.standard_normal((D, T)) / np.sqrt(D) / s[:, None] * r
    bias = 0.4 * np.random.standard_normal(T) * r
    pool = np.random.standard_normal((T, C)) / np.sqrt(T) / r[:, None]
    pool_words, pool_scales = pack4(pool)
    conf = 1 + 0.1 * np.random.standard_normal(S)
    return {"f1": bf(f1), "f2": bf(f2), "bias": bf(bias),
            "pool_words": pool_words, "pool_scales": pool_scales,
            "conf": bf(conf)}


def core(f1, f2, bias, pool_words, pool_scales, conf):
    corr = mxq(f64(f2), 0, "e4m3").T @ mxq(f64(f1), 0, "e4m3")
    h = np.maximum(corr + f64(bias)[:, None], 0.0)
    y = mxq(h, 0, "e4m3").T @ unpack4(pool_words, pool_scales)
    return y * f64(conf)[:, None]


def e4m3fn_bytes(y):
    return np.clip(np.asarray(y, np.float64), -448.0, 448.0).astype(np.float32).astype(ml_dtypes.float8_e4m3fn).view(np.uint8)


def e4m3fn_values(b):
    return np.asarray(b, np.uint8).view(ml_dtypes.float8_e4m3fn).astype(np.float64)


def setup_inputs():
    d = draw0()
    x0 = np.asarray(d['f1']).astype(np.float64)
    s = (np.max(np.abs(x0), axis=(1,), keepdims=True) / 448.0).astype(np.float32)
    out = {}
    for k, v in d.items():
        if k == 'f1':
            out['f1_bytes'] = e4m3fn_bytes(x0 / s.astype(np.float64))
            out['f1_scale'] = s
        else:
            out[k] = v
    return out


def reference(f1_bytes, f1_scale, f2, bias, pool_words, pool_scales, conf):
    return core(e4m3fn_values(f1_bytes) * f1_scale.astype(np.float64), f2, bias, pool_words, pool_scales, conf)

@@ -1,0 +1,337 @@
+from contextlib import ExitStack
+
+import concourse.mybir as mybir
+from concourse.masks import make_identity
+
+D, S, T, C = 512, 2048, 2048, 640
+FLOPS = 2 * D * S * T + 2 * S * T * C
+
+F32 = mybir.dt.float32
+BF16 = mybir.dt.bfloat16
+U32 = mybir.dt.uint32
+I32 = mybir.dt.int32
+U8 = mybir.dt.uint8
+FP8 = mybir.dt.float8_e4m3fn
+FP8X4 = mybir.dt.float8_e4m3fn_x4
+FP4X4 = mybir.dt.float4_e2m1fn_x4
+ACT = mybir.ActivationFunctionType
+ALU = mybir.AluOpType
+
+P = 128
+G = T // 512
+
+
+def tile_raft_pyramid_pooling_s13_kernel(tc, f1_bytes, f1_scale, f2, bias, pool_words, pool_scales, conf, out):
+    nc = tc.nc
+    with ExitStack() as ctx:
+        keep = ctx.enter_context(tc.tile_pool(name="keep", bufs=1))
+        work = ctx.enter_context(tc.tile_pool(name="work", bufs=3))
+        ring = ctx.enter_context(tc.psum_pool(name="ring", bufs=3))
+        ypool = ctx.enter_context(tc.psum_pool(name="ypool", bufs=1))
+
+        ctx.enter_context(tc.manual_schedule())
+
+        f1s = keep.tile([P, 4], F32, name="f1s")
+        nc.scalar.dma_start(out=f1s[:], in_=f1_scale.rearrange("(p c) o -> p (c o)", c=4))
+        bias_b = keep.tile([P, G, 4], BF16, name="bias_b")
+        nc.scalar.dma_start(out=bias_b[:], in_=bias.rearrange("(g p j) -> p g j", p=P, j=4))
+
+        f1v = f1_bytes.rearrange("(p c) s -> p c s", c=4)
+        f2v = f2.rearrange("(p c) t -> p c t", c=4)
+        f1r0 = keep.tile([P, 4, 512], U8, name="f1r0")
+        nc.sync.dma_start(out=f1r0[:], in_=f1v[:, :, 0:512])
+        f2r = []
+
+        def load_f2(g):
+            t = keep.tile([P, 4, 512], BF16, name=f"f2r{g}")
+            nc.sync.dma_start(out=t[:], in_=f2v[:, :, 512 * g : 512 * (g + 1)])
+            f2r.append(t)
+
+        load_f2(0)
+        f1r1 = keep.tile([P, 4, 512], U8, name="f1r1")
+        nc.sync.dma_start(out=f1r1[:], in_=f1v[:, :, 512:1024])
+        load_f2(1)
+        load_f2(2)
+        load_f2(3)
+        ww = keep.tile([P, G, 1280], U8, name="ww", align_bytes=64)
+        nc.sync.dma_start(out=ww[:], in_=pool_words.rearrange("g p b -> p g b"))
+        ws = keep.tile([P, G, C], U8, name="ws", align_bytes=64)
+        ws32 = ws[:].rearrange("p g n -> p (g n)").bitcast(I32)
+        nc.vector.memset(ws32, 0)
+        for q in range(4):
+            nc.sync.dma_start(
+                out=ws32[32 * q : 32 * q + 4, :].rearrange("p (g n) -> p g n", g=G),
+                in_=pool_scales.bitcast(I32)[:, 4 * q : 4 * q + 4, :].rearrange("g r n -> r g n"),
+            )
+        f1r2 = keep.tile([P, 4, 1024], U8, name="f1r2")
+        nc.sync.dma_start(out=f1r2[:], in_=f1v[:, :, 1024:2048])
+        ident = keep.tile([P, P], BF16, name="ident")
+        make_identity(nc, ident[:])
+        bias_t = keep.tile([P, G, 4], F32, name="bias_t")
+        nc.gpsimd.tensor_copy(out=bias_t[:], in_=bias_b[:])
+        cz = keep.tile([P, P], BF16, name="cz")
+        nc.gpsimd.memset(cz[:], 0.0)
+        nc.sync.dma_start(out=cz[0:16, :], in_=conf.rearrange("(i p) -> i p", p=P))
+
+        dummy = keep.tile([P, 1], F32, name="dummy")
+        nc.vector.memset(dummy[:], 0.0)
+        nc.scalar.activation(out=dummy[:], in_=dummy[:], func=ACT.Relu)
+
+        f1w, f1i, f1c, f1p = {}, {}, {}, {}
+
+        def f1_widen(c, eng, t):
+            if c not in f1w:
+                f1w[c] = work.tile([P, 4, 512], BF16, name="f1w")
+            raw = (f1r0[:, t, :], f1r1[:, t, :], f1r2[:, t, 0:512], f1r2[:, t, 512:1024])[c]
+            if eng == "s":
+                nc.scalar.activation(out=f1w[c][:, t, :], in_=raw.bitcast(FP8), func=ACT.Copy, scale=f1s[:, t : t + 1])
+            else:
+                nc.vector.tensor_scalar(out=f1w[c][:, t, :], in0=raw.bitcast(FP8), scalar1=f1s[:, t : t + 1], scalar2=None, op0=ALU.mult)
+
+        def interleave(dst, src, h, n):
+            nc.vector.tensor_copy(
+                out=dst[:, n * h : n * (h + 1), :].rearrange("p (b i) t -> p b t i", i=4),
+                in_=src[:, :, n * h : n * (h + 1)].rearrange("p t (b i) -> p b t i", i=4),
+            )
+
+        def quant(codes, scales, src, h, n):
+            nc.vector.quantize_mx(
+                out=codes[:, n * h : n * (h + 1)].bitcast(FP8X4),
+                scales=scales[:, n * h : n * (h + 1)],
+                in_=src[:, n * h : n * (h + 1), :].rearrange("p n t -> p (n t)"),
+            )
+
+        def f1_inter(c, h, n=256):
+            if c not in f1i:
+                f1i[c] = work.tile([P, 512, 4], BF16, name="f1i", align_bytes=64)
+            interleave(f1i[c], f1w[c], h, n)
+
+        def f1_quant(c, h, n=256):
+            if c not in f1c:
+                f1c[c] = keep.tile([P, 512], U32, name=f"f1c{c}", align_bytes=64)
+                f1p[c] = keep.tile([P, 512], U8, name=f"f1p{c}", align_bytes=64)
+            quant(f1c[c], f1p[c], f1i[c], h, n)
+
+        f2i, f2c, f2p = {}, {}, {}
+
+        f2ps = {}
+
+        def f2_pe(g, h):
+            ps = ypool.tile([P, 1024], BF16, name=f"y{(2 * g + h) % 4}")
+            f2ps[g, h] = ps
+            for jj in range(2):
+                j = 2 * h + jj
+                nc.tensor.matmul(
+                    out=ps[:, 512 * jj : 512 * (jj + 1)],
+                    lhsT=ident[:],
+                    rhs=f2r[g][:].rearrange("p c (m j) -> p j m c", j=4)[:, j],
+                    start=True,
+                    stop=True,
+                )
+
+        def f2_copy(g, h):
+            if g not in f2i:
+                f2i[g] = work.tile([P, 512, 4], BF16, name="f2i", align_bytes=64)
+            nc.scalar.copy(out=f2i[g][:, 256 * h : 256 * (h + 1), :].rearrange("p n t -> p (n t)"), in_=f2ps[g, h][:])
+
+        def f2_quant(g, h):
+            if g not in f2c:
+                f2c[g] = keep.tile([P, 512], U32, name=f"f2c{g}", align_bytes=64)
+                f2p[g] = keep.tile([P, 512], U8, name=f"f2p{g}", align_bytes=64)
+            quant(f2c[g], f2p[g], f2i[g], h, 256)
+
+        hp, hi, hc, hs = {}, {}, {}, {}
+
+        corr = {}
+
+        def a_mm(u, j, n0=0, n1=512):
+            c, g = divmod(u, G)
+            ps = ring.tile([P, n1 - n0], F32, name="corr")
+            corr[u, j] = ps
+            nc.tensor.matmul_mx(
+                out=ps[:],
+                lhsT=f2c[g][:, 128 * j : 128 * (j + 1)].bitcast(FP8X4),
+                lhsT_scale=f2p[g][:, 128 * j : 128 * (j + 1)],
+                rhs=f1c[c][:, n0:n1].bitcast(FP8X4),
+                rhs_scale=f1p[c][:, n0:n1],
+                start=True,
+                stop=True,
+            )
+
+        def a_act(u, j, n0=0, n1=512):
+            c, g = divmod(u, G)
+            if u not in hp:
+                hp[u] = work.tile([P, 4, 512], BF16, name="hp")
+            nc.scalar.activation(out=hp[u][:, j, n0:n1], in_=corr[u, j][:], func=ACT.Relu, bias=bias_t[:, g, j : j + 1])
+
+        def h_inter(u, h, n=256):
+            if u not in hi:
+                hi[u] = work.tile([P, 512, 4], BF16, name="hi", align_bytes=64)
+            interleave(hi[u], hp[u], h, n)
+
+        def h_quant(u, h, n=256):
+            if u not in hc:
+                hc[u] = keep.tile([P, 512], U32, name=f"hc{u}", align_bytes=64)
+                hs[u] = keep.tile([P, 512], U8, name=f"hs{u}", align_bytes=64)
+            quant(hc[u], hs[u], hi[u], h, n)
+
+        ybig, ysml, osb = {}, {}, {}
+
+        def b_mm(u, k, ps, n0, n1, start, stop):
+            g = u % G
+            nc.tensor.matmul_mx(
+                out=ps,
+                lhsT=hc[u][:, 128 * k : 128 * (k + 1)].bitcast(FP8X4),
+                lhsT_scale=hs[u][:, 128 * k : 128 * (k + 1)],
+                rhs=ww[:, g, 2 * n0 : 2 * n1].bitcast(FP4X4),
+                rhs_scale=ws[:, g, n0:n1],
+                start=start,
+                stop=stop,
+            )
+
+        def b_big(u, k):
+            c, g = divmod(u, G)
+            if g == 0:
+                ybig[c, k] = ypool.tile([P, 512], F32, name=f"y{k}")
+            b_mm(u, k, ybig[c, k][:], 0, 512, g == 0, g == G - 1)
+
+        def e_sml(c, k):
+            if c not in ysml:
+                ysml[c] = ypool.tile([P, 4, 128], F32, name="ys")
+            for g in range(G):
+                b_mm(c * G + g, k, ysml[c][:, k, :], 512, 640, g == 0, g == G - 1)
+
+        def o_tile(c, k):
+            if c not in osb:
+                osb[c] = work.tile([P, 4, C], F32, name="osb", bufs=2)
+            return osb[c][:, k, :]
+
+        def y_out(c, k, eng, ps, n0, n1):
+            o = o_tile(c, k)
+            cf = conf_t[:, 4 * c + k : 4 * c + k + 1]
+            if eng == "s":
+                nc.scalar.activation(out=o[:, n0:n1], in_=ps, func=ACT.Copy, scale=cf)
+            else:
+                nc.vector.tensor_scalar(out=o[:, n0:n1], in0=ps, scalar1=cf, scalar2=None, op0=ALU.mult)
+
+        def y_small(c):
+            o_tile(c, 0)
+            nc.vector.tensor_tensor(
+                out=osb[c][:, :, 512:640],
+                in0=ysml[c][:],
+                in1=conf_t[:, 4 * c : 4 * c + 4].unsqueeze(2).to_broadcast([P, 4, 128]),
+                op=ALU.mult,
+            )
+
+        def store(c, k):
+            r0 = 512 * c + 128 * k
+            nc.sync.dma_start(out=out[r0 : r0 + 128, :], in_=osb[c][:, k, :])
+
+        f1_widen(0, "s", 0)
+        f1_widen(0, "v", 1)
+        f1_widen(0, "v", 2)
+        f1_widen(0, "v", 3)
+        f2_pe(0, 0)
+        f2_pe(0, 1)
+        f1_inter(0, 0)
+        f1_inter(0, 1)
+        f2_copy(0, 0)
+        f2_copy(0, 1)
+        f2_pe(1, 0)
+        f2_pe(1, 1)
+        f1_widen(1, "s", 0)
+        f1_quant(0, 0)
+        f1_quant(0, 1)
+        f2_quant(0, 0)
+        f2_quant(0, 1)
+        f2_copy(1, 0)
+        f2_copy(1, 1)
+        f2_quant(1, 0)
+        f2_quant(1, 1)
+
+        LAG = 2
+        SN = (4, 3, 2)
+        for u in range(16 + LAG):
+            c, g = divmod(u, G)
+            v = u - LAG
+            ce = v // G - 1 if v >= 0 else -1
+            ee = v >= 0 and v % G == 0 and v >= G
+            en = v >= 0 and v % G == 1 and v >= G
+            for j in range(4):
+                if ee and j < SN[ce]:
+                    y_out(ce, j, "s", ybig[ce, j][:], 0, 512)
+                if u < 15:
+                    a_mm(u, j)
+                    a_act(u, j)
+                elif u == 15:
+                    a_mm(u, j, 0, 256)
+                    a_act(u, j, 0, 256)
+                if u < 2 and j % 2 == 0:
+                    f2_pe(u + 2, j // 2)
+                    f2_copy(u + 2, j // 2)
+                if ee:
+                    e_sml(ce, j)
+                elif en:
+                    b_big(v - 1, j)
+                    b_big(v, j)
+                elif v >= 0 and v < 15:
+                    b_big(v, j)
+            if u == 0:
+                for t in range(1, 4):
+                    f1_widen(1, "v", t)
+                f1_inter(1, 0)
+                f1_inter(1, 1)
+            if u < 2:
+                f2_quant(u + 2, 0)
+                f2_quant(u + 2, 1)
+            if u == 0:
+                f1_quant(1, 0)
+                f1_quant(1, 1)
+            if u == 3:
+                tp = ypool.tile([P, P], BF16, name="ys")
+                nc.tensor.transpose(tp[:], cz[:], ident[:])
+                conf_t = keep.tile([P, 16], F32, name="conf_t")
+                nc.scalar.copy(out=conf_t[:], in_=tp[:, 0:16])
+            if ee:
+                for k in range(SN[ce], 4):
+                    y_out(ce, k, "v", ybig[ce, k][:], 0, 512)
+            if u < 16:
+                if g == 0 and 0 < c < 3:
+                    for t in range(4):
+                        f1_widen(c + 1, "v", t)
+                if g == 1 and 0 < c < 3:
+                    f1_inter(c + 1, 0)
+                    f1_inter(c + 1, 1)
+                if g == 2 and 0 < c < 3:
+                    f1_quant(c + 1, 0)
+                    f1_quant(c + 1, 1)
+                if u == 15:
+                    for j in range(4):
+                        a_mm(u, j, 256, 512)
+                        a_act(u, j, 256, 512)
+                    h_inter(u, 0)
+                    h_quant(u, 0)
+                    h_inter(u, 1)
+                    h_quant(u, 1)
+                else:
+                    h_inter(u, 0)
+                    h_inter(u, 1)
+                    h_quant(u, 0)
+                    h_quant(u, 1)
+            if ee:
+                y_small(ce)
+                for k in range(4):
+                    store(ce, k)
+        sm = [ypool.tile([P, 128], F32, name="ys")]
+        for k in range(1, 4):
+            t = ring.tile([P, 128], F32, name="corr")
+            sm.append(t)
+        for g in range(3):
+            for k in range(4):
+                b_mm(12 + g, k, sm[k][:], 512, 640, g == 0, False)
+        for k in range(4):
+            b_big(15, k)
+            b_mm(15, k, sm[k][:], 512, 640, False, True)
+            y_out(3, k, "s" if k < 2 else "v" if k==2 else "s", ybig[3, k][:], 0, 512)
+            y_out(3, k, "v" if k < 2 else "s" if k==2 else "v", sm[k][:], 512, 640)
+            store(3, k)

@@ -114,25 +114,15 @@ def tile_raft_pyramid_pooling_s13_kernel(tc, f1_bytes, f1_scale, f2, bias, pool_
 
         f2i, f2c, f2p = {}, {}, {}
 
-        f2ps = {}
-
-        def f2_pe(g, h):
-            ps = ypool.tile([P, 1024], BF16, name=f"y{(2 * g + h) % 4}")
-            f2ps[g, h] = ps
-            for jj in range(2):
-                j = 2 * h + jj
-                nc.tensor.matmul(
-                    out=ps[:, 512 * jj : 512 * (jj + 1)],
-                    lhsT=ident[:],
-                    rhs=f2r[g][:].rearrange("p c (m j) -> p j m c", j=4)[:, j],
-                    start=True,
-                    stop=True,
-                )
-
-        def f2_copy(g, h):
+        def f2_inter(g, h, eng):
             if g not in f2i:
                 f2i[g] = work.tile([P, 512, 4], BF16, name="f2i", align_bytes=64)
-            nc.scalar.copy(out=f2i[g][:, 256 * h : 256 * (h + 1), :].rearrange("p n t -> p (n t)"), in_=f2ps[g, h][:])
+            dst = f2i[g][:, 256 * h : 256 * (h + 1), :].rearrange("p (j m) c -> p m c j", j=2)
+            src = f2r[g][:].rearrange("p c (m j) -> p m c j", j=4)[:, :, :, 2 * h : 2 * h + 2]
+            if eng == "s":
+                nc.scalar.copy(out=dst, in_=src)
+            else:
+                nc.vector.tensor_copy(out=dst, in_=src)
 
         def f2_quant(g, h):
             if g not in f2c:
@@ -231,26 +221,21 @@ def tile_raft_pyramid_pooling_s13_kernel(tc, f1_bytes, f1_scale, f2, bias, pool_
         f1_widen(0, "v", 1)
         f1_widen(0, "v", 2)
         f1_widen(0, "v", 3)
-        f2_pe(0, 0)
-        f2_pe(0, 1)
         f1_inter(0, 0)
         f1_inter(0, 1)
-        f2_copy(0, 0)
-        f2_copy(0, 1)
-        f2_pe(1, 0)
-        f2_pe(1, 1)
-        f1_widen(1, "s", 0)
+        f2_inter(0, 0, "v")
+        f2_inter(0, 1, "s")
         f1_quant(0, 0)
         f1_quant(0, 1)
         f2_quant(0, 0)
         f2_quant(0, 1)
-        f2_copy(1, 0)
-        f2_copy(1, 1)
+        f2_inter(1, 0, "v")
+        f2_inter(1, 1, "s")
         f2_quant(1, 0)
         f2_quant(1, 1)
 
         LAG = 2
-        SN = (4, 3, 2)
+        SN = (3, 3, 1)
         for u in range(16 + LAG):
             c, g = divmod(u, G)
             v = u - LAG
@@ -266,9 +251,16 @@ def tile_raft_pyramid_pooling_s13_kernel(tc, f1_bytes, f1_scale, f2, bias, pool_
                 elif u == 15:
                     a_mm(u, j, 0, 256)
                     a_act(u, j, 0, 256)
-                if u < 2 and j % 2 == 0:
-                    f2_pe(u + 2, j // 2)
-                    f2_copy(u + 2, j // 2)
+                if (u, j) in ((0, 0),):
+                    f2_inter(2, 1, "s")
+                if (u, j) in ((0, 3),):
+                    f2_inter(3, 1, "s")
+                if (u, j) in ((0, 1), (0, 3), (1, 1), (1, 2)):
+                    f1_widen(1, "s", ((0, 1), (0, 3), (1, 1), (1, 2)).index((u, j)))
+                if u == 2 and j < 2:
+                    f1_widen(2, "s", j)
+                if u == 3 and j < 2:
+                    f1_widen(3, "s", j)
                 if ee:
                     e_sml(ce, j)
                 elif en:
@@ -277,16 +269,13 @@ def tile_raft_pyramid_pooling_s13_kernel(tc, f1_bytes, f1_scale, f2, bias, pool_
                 elif v >= 0 and v < 15:
                     b_big(v, j)
             if u == 0:
-                for t in range(1, 4):
-                    f1_widen(1, "v", t)
-                f1_inter(1, 0)
-                f1_inter(1, 1)
-            if u < 2:
-                f2_quant(u + 2, 0)
-                f2_quant(u + 2, 1)
-            if u == 0:
-                f1_quant(1, 0)
-                f1_quant(1, 1)
+                f2_inter(2, 0, "v")
+                f2_quant(2, 0)
+                f2_quant(2, 1)
+            if u == 1:
+                f2_inter(3, 0, "v")
+                f2_quant(3, 0)
+                f2_quant(3, 1)
             if u == 3:
                 tp = ypool.tile([P, P], BF16, name="ys")
                 nc.tensor.transpose(tp[:], cz[:], ident[:])
@@ -297,12 +286,12 @@ def tile_raft_pyramid_pooling_s13_kernel(tc, f1_bytes, f1_scale, f2, bias, pool_
                     y_out(ce, k, "v", ybig[ce, k][:], 0, 512)
             if u < 16:
                 if g == 0 and 0 < c < 3:
-                    for t in range(4):
+                    for t in range(2 if c == 1 else 2, 4):
                         f1_widen(c + 1, "v", t)
-                if g == 1 and 0 < c < 3:
+                if g == 1 and 0 < c < 3 or u == 2:
                     f1_inter(c + 1, 0)
                     f1_inter(c + 1, 1)
-                if g == 2 and 0 < c < 3:
+                if g == 2 and 0 < c < 3 or u == 2:
                     f1_quant(c + 1, 0)
                     f1_quant(c + 1, 1)
                 if u == 15:

@@ -18,6 +18,7 @@ ACT = mybir.ActivationFunctionType
 ALU = mybir.AluOpType
 
 P = 128
+CFG = {"p":[["v",-6],["s",-5],["v",-5],["v",-6],["v",-4],["s",-2],["v",-4],["v",0]],"pq":[-5,-3,-2,4],"w":[["v",-9],["v",-9],["s",-9],["v",-9],["s",0],["s",-4],["s",-4],["s",-5],["s",9],["s",14],["s",8],["s",10],["v",13],["v",14],["v",16],["v",14]],"fi":[-9,4,8,20],"fq":[-8,5,12,20],"y":[["s",26],["s",25],["v",12],["s",28],["s",41],["s",40],["s",44],["s",43],["s",56],["v",28],["s",60],["v",28]],"ys":[["v",16],["v",22],["s",63]],"lag":2,"bj":4,"sec":[[0,4],[1,5],[2,6],[3,7]],"vu":[],"half":[15],"end":["sv","vs","vs","vs"],"tv":[]}
 G = T // 512
 
 
@@ -165,6 +166,39 @@ def tile_raft_pyramid_pooling_s13_kernel(tc, f1_bytes, f1_scale, f2, bias, pool_
                 hs[u] = keep.tile([P, 512], U8, name=f"hs{u}", align_bytes=64)
             quant(hc[u], hs[u], hi[u], h, n)
 
+        def bias_grid(g):
+            return bias_t[:, g, :].unsqueeze(1).to_broadcast([P, 128, 4])
+
+        def v_mm(u, n):
+            c, g = divmod(u, G)
+            ps = ring.tile([P, 4, 128], F32, name="corr")
+            corr[u, "v", n] = ps
+            for j in range(4):
+                nc.tensor.matmul_mx(
+                    out=ps[:, j, :],
+                    lhsT=f2c[g][:, 128 * j : 128 * (j + 1)].bitcast(FP8X4),
+                    lhsT_scale=f2p[g][:, 128 * j : 128 * (j + 1)],
+                    rhs=f1c[c][:, 128 * n : 128 * (n + 1)].bitcast(FP8X4),
+                    rhs_scale=f1p[c][:, 128 * n : 128 * (n + 1)],
+                    start=True,
+                    stop=True,
+                )
+
+        def v_add(u, n):
+            g = u % G
+            if u not in hi:
+                hi[u] = work.tile([P, 512, 4], BF16, name="hi", align_bytes=64)
+            nc.vector.tensor_tensor(
+                out=hi[u][:, 128 * n : 128 * (n + 1), :],
+                in0=corr[u, "v", n][:].rearrange("p j n -> p n j"),
+                in1=bias_grid(g),
+                op=ALU.add,
+            )
+
+        def v_relu(u, h):
+            flat = hi[u][:, 256 * h : 256 * (h + 1), :].rearrange("p n t -> p (n t)")
+            nc.vector.tensor_scalar(out=flat, in0=flat, scalar1=0.0, scalar2=None, op0=ALU.max)
+
         ybig, ysml, osb = {}, {}, {}
 
         def b_mm(u, k, ps, n0, n1, start, stop):
@@ -185,11 +219,10 @@ def tile_raft_pyramid_pooling_s13_kernel(tc, f1_bytes, f1_scale, f2, bias, pool_
                 ybig[c, k] = ypool.tile([P, 512], F32, name=f"y{k}")
             b_mm(u, k, ybig[c, k][:], 0, 512, g == 0, g == G - 1)
 
-        def e_sml(c, k):
+        def b_sml(c, k, g):
             if c not in ysml:
                 ysml[c] = ypool.tile([P, 4, 128], F32, name="ys")
-            for g in range(G):
-                b_mm(c * G + g, k, ysml[c][:, k, :], 512, 640, g == 0, g == G - 1)
+            b_mm(c * G + g, k, ysml[c][:, k, :], 512, 640, g == 0, g == G - 1)
 
         def o_tile(c, k):
             if c not in osb:
@@ -217,100 +250,127 @@ def tile_raft_pyramid_pooling_s13_kernel(tc, f1_bytes, f1_scale, f2, bias, pool_
             r0 = 512 * c + 128 * k
             nc.sync.dma_start(out=out[r0 : r0 + 128, :], in_=osb[c][:, k, :])
 
-        f1_widen(0, "s", 0)
-        f1_widen(0, "v", 1)
-        f1_widen(0, "v", 2)
-        f1_widen(0, "v", 3)
-        f1_inter(0, 0)
-        f1_inter(0, 1)
-        f2_inter(0, 0, "v")
-        f2_inter(0, 1, "s")
-        f1_quant(0, 0)
-        f1_quant(0, 1)
-        f2_quant(0, 0)
-        f2_quant(0, 1)
-        f2_inter(1, 0, "v")
-        f2_inter(1, 1, "s")
-        f2_quant(1, 0)
-        f2_quant(1, 1)
+        S_AT, V_AT = {}, {}
 
-        LAG = 2
-        SN = (3, 3, 1)
+        def at(eng, pos, fn, *args):
+            (S_AT if eng == "s" else V_AT).setdefault(pos, []).append((fn, args))
+
+        for g in range(G):
+            for h in range(2):
+                e, pos = CFG["p"][2 * g + h]
+                at(e, pos, f2_inter, g, h, e)
+            if CFG["pq"][g] is not None:
+                at("v", CFG["pq"][g], f2_quant, g, 0)
+                at("v", CFG["pq"][g], f2_quant, g, 1)
+        for c in range(4):
+            for t in range(4):
+                e, pos = CFG["w"][4 * c + t]
+                at(e, pos, f1_widen, c, e, t)
+            for h in range(2):
+                at("v", CFG["fi"][c], f1_inter, c, h)
+            for h in range(2):
+                at("v", CFG["fq"][c], f1_quant, c, h)
+
+        def ybig_out(c, k, e):
+            y_out(c, k, e, ybig[c, k][:], 0, 512)
+
+        def small_out(c, e):
+            if e == "v":
+                y_small(c)
+            else:
+                for k in range(4):
+                    y_out(c, k, "s", ysml[c][:, k, :], 512, 640)
+            for k in range(4):
+                store(c, k)
+
+        for c in range(3):
+            for k in range(4):
+                e, pos = CFG["y"][4 * c + k]
+                at(e, pos, ybig_out, c, k, e)
+            e, pos = CFG["ys"][c]
+            at(e, pos, small_out, c, e)
+
+        def go(d, pos):
+            for fn, args in d.get(pos, ()):
+                fn(*args)
+
+        tp = ypool.tile([P, P], BF16, name="ys")
+        conf_t = keep.tile([P, 16], F32, name="conf_t")
+        for i in range(-9, 0):
+            go(S_AT, i)
+            go(V_AT, i)
+        LAG = CFG["lag"]
+        VU = CFG["vu"]
+        HALF = CFG["half"]
         for u in range(16 + LAG):
-            c, g = divmod(u, G)
             v = u - LAG
-            ce = v // G - 1 if v >= 0 else -1
-            ee = v >= 0 and v % G == 0 and v >= G
-            en = v >= 0 and v % G == 1 and v >= G
+            cv, gv = divmod(v, G)
+            first = v >= G and gv == 0
+            second = v >= G and gv == 1
             for j in range(4):
-                if ee and j < SN[ce]:
-                    y_out(ce, j, "s", ybig[ce, j][:], 0, 512)
-                if u < 15:
-                    a_mm(u, j)
-                    a_act(u, j)
-                elif u == 15:
-                    a_mm(u, j, 0, 256)
-                    a_act(u, j, 0, 256)
-                if (u, j) in ((0, 0),):
-                    f2_inter(2, 1, "s")
-                if (u, j) in ((0, 3),):
-                    f2_inter(3, 1, "s")
-                if (u, j) in ((0, 1), (0, 3), (1, 1), (1, 2)):
-                    f1_widen(1, "s", ((0, 1), (0, 3), (1, 1), (1, 2)).index((u, j)))
-                if u == 2 and j < 2:
-                    f1_widen(2, "s", j)
-                if u == 3 and j < 2:
-                    f1_widen(3, "s", j)
-                if ee:
-                    e_sml(ce, j)
-                elif en:
-                    b_big(v - 1, j)
+                go(S_AT, 4 * u + j)
+                if u < 16:
+                    if u in VU:
+                        v_mm(u, j)
+                    elif u in HALF:
+                        a_mm(u, j, 0, 256)
+                        a_act(u, j, 0, 256)
+                    else:
+                        a_mm(u, j)
+                        a_act(u, j)
+                if first:
+                    for g in range(G):
+                        b_sml(cv - 1, j, g)
+                    if j >= CFG["bj"]:
+                        b_big(v, j - CFG["bj"])
+                elif second:
+                    for i in CFG["sec"][j]:
+                        b_big(v - 1 if i < 4 else v, i % 4)
+                elif 0 <= v < 15:
                     b_big(v, j)
-                elif v >= 0 and v < 15:
-                    b_big(v, j)
-            if u == 0:
-                f2_inter(2, 0, "v")
-                f2_quant(2, 0)
-                f2_quant(2, 1)
-            if u == 1:
-                f2_inter(3, 0, "v")
-                f2_quant(3, 0)
-                f2_quant(3, 1)
-            if u == 3:
-                tp = ypool.tile([P, P], BF16, name="ys")
+            if u == 2:
                 nc.tensor.transpose(tp[:], cz[:], ident[:])
-                conf_t = keep.tile([P, 16], F32, name="conf_t")
                 nc.scalar.copy(out=conf_t[:], in_=tp[:, 0:16])
-            if ee:
-                for k in range(SN[ce], 4):
-                    y_out(ce, k, "v", ybig[ce, k][:], 0, 512)
-            if u < 16:
-                if g == 0 and 0 < c < 3:
-                    for t in range(2 if c == 1 else 2, 4):
-                        f1_widen(c + 1, "v", t)
-                if g == 1 and 0 < c < 3 or u == 2:
-                    f1_inter(c + 1, 0)
-                    f1_inter(c + 1, 1)
-                if g == 2 and 0 < c < 3 or u == 2:
-                    f1_quant(c + 1, 0)
-                    f1_quant(c + 1, 1)
-                if u == 15:
-                    for j in range(4):
-                        a_mm(u, j, 256, 512)
-                        a_act(u, j, 256, 512)
-                    h_inter(u, 0)
+            if u in CFG["tv"]:
+                v_mm(u, 2)
+                v_mm(u, 3)
+            elif u in HALF:
+                for j in range(4):
+                    a_mm(u, j, 256, 512)
+                    a_act(u, j, 256, 512)
+            go(V_AT, 2 * u)
+            if u in VU:
+                v_add(u, 0)
+                v_add(u, 1)
+                v_add(u, 2)
+                v_relu(u, 0)
+                v_add(u, 3)
+                h_quant(u, 0)
+                v_relu(u, 1)
+                go(V_AT, 2 * u + 1)
+                h_quant(u, 1)
+            elif u in CFG["tv"]:
+                v_add(u, 2)
+                v_add(u, 3)
+                v_relu(u, 1)
+                h_inter(u, 0)
+                h_quant(u, 1)
+                go(V_AT, 2 * u + 1)
+                h_quant(u, 0)
+            elif u < 16:
+                h_inter(u, 0)
+                if u in HALF:
                     h_quant(u, 0)
                     h_inter(u, 1)
+                    go(V_AT, 2 * u + 1)
                     h_quant(u, 1)
                 else:
-                    h_inter(u, 0)
                     h_inter(u, 1)
+                    go(V_AT, 2 * u + 1)
                     h_quant(u, 0)
                     h_quant(u, 1)
-            if ee:
-                y_small(ce)
-                for k in range(4):
-                    store(ce, k)
+            else:
+                go(V_AT, 2 * u + 1)
         sm = [ypool.tile([P, 128], F32, name="ys")]
         for k in range(1, 4):
             t = ring.tile([P, 128], F32, name="corr")
@@ -321,6 +381,9 @@ def tile_raft_pyramid_pooling_s13_kernel(tc, f1_bytes, f1_scale, f2, bias, pool_
         for k in range(4):
             b_big(15, k)
             b_mm(15, k, sm[k][:], 512, 640, False, True)
-            y_out(3, k, "s" if k < 2 else "v" if k==2 else "s", ybig[3, k][:], 0, 512)
-            y_out(3, k, "v" if k < 2 else "s" if k==2 else "v", sm[k][:], 512, 640)
-            store(3, k)
+            e1, e2 = CFG["end"][k]
+            y_out(3, k, e1, ybig[3, k][:], 0, 512)
+            y_out(3, k, e2, sm[k][:], 512, 640)
+            r0 = 1536 + 128 * k
+            nc.sync.dma_start(out=out[r0 : r0 + 128, 0:512], in_=osb[3][:, k, 0:512])
+            nc.sync.dma_start(out=out[r0 : r0 + 128, 512:640], in_=osb[3][:, k, 512:640])

@@ -18,372 +18,352 @@ ACT = mybir.ActivationFunctionType
 ALU = mybir.AluOpType
 
 P = 128
-CFG = {"p":[["v",-6],["s",-5],["v",-5],["v",-6],["v",-4],["s",-2],["v",-4],["v",0]],"pq":[-5,-3,-2,4],"w":[["v",-9],["v",-9],["s",-9],["v",-9],["s",0],["s",-4],["s",-4],["s",-5],["s",9],["s",14],["s",8],["s",10],["v",13],["v",14],["v",16],["v",14]],"fi":[-9,4,8,20],"fq":[-8,5,12,20],"y":[["s",26],["s",25],["v",12],["s",28],["s",41],["s",40],["s",44],["s",43],["s",56],["v",28],["s",60],["v",28]],"ys":[["v",16],["v",22],["s",63]],"lag":2,"bj":4,"sec":[[0,4],[1,5],[2,6],[3,7]],"vu":[],"half":[15],"end":["sv","vs","vs","vs"],"tv":[]}
-G = T // 512
+PACK = 4
+N = 512
+HALF = N // 2
+GROUPS = T // N
+CHUNKS = S // N
+UNITS = GROUPS * CHUNKS
+TILES = N // P
+FINE = 512
+LAG = 2
+
+WIDEN_2_SLOTS = (10, 12, 14, 16)
+WIDEN_3_SLOT = 26
+SUM_SLOT = (24, 40, 57)
+SUM_TILES = (3, 3, 2)
 
 
-def tile_raft_pyramid_pooling_s13_kernel(tc, f1_bytes, f1_scale, f2, bias, pool_words, pool_scales, conf, out):
+def tile_raft_pyramid_pooling_s13_kernel(
+    tc, f1_bytes, f1_scale, f2, bias, pool_words, pool_scales, conf, out
+):
     nc = tc.nc
     with ExitStack() as ctx:
         keep = ctx.enter_context(tc.tile_pool(name="keep", bufs=1))
         work = ctx.enter_context(tc.tile_pool(name="work", bufs=3))
         ring = ctx.enter_context(tc.psum_pool(name="ring", bufs=3))
-        ypool = ctx.enter_context(tc.psum_pool(name="ypool", bufs=1))
-
+        sums = ctx.enter_context(tc.psum_pool(name="sums", bufs=1))
         ctx.enter_context(tc.manual_schedule())
 
-        f1s = keep.tile([P, 4], F32, name="f1s")
-        nc.scalar.dma_start(out=f1s[:], in_=f1_scale.rearrange("(p c) o -> p (c o)", c=4))
-        bias_b = keep.tile([P, G, 4], BF16, name="bias_b")
-        nc.scalar.dma_start(out=bias_b[:], in_=bias.rearrange("(g p j) -> p g j", p=P, j=4))
+        f1_factor = keep.tile([P, PACK], F32, name="f1_factor")
+        nc.scalar.dma_start(out=f1_factor[:], in_=f1_scale.rearrange("(p c) o -> p (c o)", c=PACK))
+        bias_bf = keep.tile([P, GROUPS, PACK], BF16, name="bias_bf")
+        nc.scalar.dma_start(out=bias_bf[:], in_=bias.rearrange("(g p j) -> p g j", p=P, j=PACK))
 
-        f1v = f1_bytes.rearrange("(p c) s -> p c s", c=4)
-        f2v = f2.rearrange("(p c) t -> p c t", c=4)
-        f1r0 = keep.tile([P, 4, 512], U8, name="f1r0")
-        nc.sync.dma_start(out=f1r0[:], in_=f1v[:, :, 0:512])
-        f2r = []
+        f1_rows = f1_bytes.rearrange("(p c) s -> p c s", c=PACK)
+        f2_rows = f2.rearrange("(p c) t -> p c t", c=PACK)
+
+        def load_f1(name, s0, s1):
+            bytes_in = keep.tile([P, PACK, s1 - s0], U8, name=name)
+            nc.sync.dma_start(out=bytes_in[:], in_=f1_rows[:, :, s0:s1])
+            return bytes_in
 
         def load_f2(g):
-            t = keep.tile([P, 4, 512], BF16, name=f"f2r{g}")
-            nc.sync.dma_start(out=t[:], in_=f2v[:, :, 512 * g : 512 * (g + 1)])
-            f2r.append(t)
+            rows = keep.tile([P, PACK, N], BF16, name=f"f2_raw{g}")
+            nc.sync.dma_start(out=rows[:], in_=f2_rows[:, :, N * g : N * (g + 1)])
+            return rows
 
-        load_f2(0)
-        f1r1 = keep.tile([P, 4, 512], U8, name="f1r1")
-        nc.sync.dma_start(out=f1r1[:], in_=f1v[:, :, 512:1024])
-        load_f2(1)
-        load_f2(2)
-        load_f2(3)
-        ww = keep.tile([P, G, 1280], U8, name="ww", align_bytes=64)
-        nc.sync.dma_start(out=ww[:], in_=pool_words.rearrange("g p b -> p g b"))
-        ws = keep.tile([P, G, C], U8, name="ws", align_bytes=64)
-        ws32 = ws[:].rearrange("p g n -> p (g n)").bitcast(I32)
-        nc.vector.memset(ws32, 0)
+        f1_raw0 = load_f1("f1_raw0", 0, N)
+        f2_raw = [load_f2(0)]
+        f1_raw1 = load_f1("f1_raw1", N, 2 * N)
+        for g in range(1, GROUPS):
+            f2_raw.append(load_f2(g))
+        words = keep.tile([P, GROUPS, 2 * C], U8, name="words", align_bytes=64)
+        nc.sync.dma_start(out=words[:], in_=pool_words.rearrange("g p b -> p g b"))
+        w_scales = keep.tile([P, GROUPS, C], U8, name="w_scales", align_bytes=64)
+        w_scales_i32 = w_scales[:].rearrange("p g n -> p (g n)").bitcast(I32)
+        nc.vector.memset(w_scales_i32, 0)
         for q in range(4):
             nc.sync.dma_start(
-                out=ws32[32 * q : 32 * q + 4, :].rearrange("p (g n) -> p g n", g=G),
+                out=w_scales_i32[32 * q : 32 * q + 4, :].rearrange("p (g n) -> p g n", g=GROUPS),
                 in_=pool_scales.bitcast(I32)[:, 4 * q : 4 * q + 4, :].rearrange("g r n -> r g n"),
             )
-        f1r2 = keep.tile([P, 4, 1024], U8, name="f1r2")
-        nc.sync.dma_start(out=f1r2[:], in_=f1v[:, :, 1024:2048])
+        f1_raw23 = load_f1("f1_raw23", 2 * N, 4 * N)
+
         ident = keep.tile([P, P], BF16, name="ident")
         make_identity(nc, ident[:])
-        bias_t = keep.tile([P, G, 4], F32, name="bias_t")
-        nc.gpsimd.tensor_copy(out=bias_t[:], in_=bias_b[:])
-        cz = keep.tile([P, P], BF16, name="cz")
-        nc.gpsimd.memset(cz[:], 0.0)
-        nc.sync.dma_start(out=cz[0:16, :], in_=conf.rearrange("(i p) -> i p", p=P))
-
+        bias_t = keep.tile([P, GROUPS, PACK], F32, name="bias_t")
+        nc.gpsimd.tensor_copy(out=bias_t[:], in_=bias_bf[:])
+        conf_rows = keep.tile([P, P], BF16, name="conf_rows")
+        nc.gpsimd.memset(conf_rows[:], 0.0)
+        nc.sync.dma_start(out=conf_rows[0 : S // P, :], in_=conf.rearrange("(i p) -> i p", p=P))
+        conf_t = keep.tile([P, S // P], F32, name="conf_t")
         dummy = keep.tile([P, 1], F32, name="dummy")
         nc.vector.memset(dummy[:], 0.0)
         nc.scalar.activation(out=dummy[:], in_=dummy[:], func=ACT.Relu)
 
-        f1w, f1i, f1c, f1p = {}, {}, {}, {}
-
-        def f1_widen(c, eng, t):
-            if c not in f1w:
-                f1w[c] = work.tile([P, 4, 512], BF16, name="f1w")
-            raw = (f1r0[:, t, :], f1r1[:, t, :], f1r2[:, t, 0:512], f1r2[:, t, 512:1024])[c]
-            if eng == "s":
-                nc.scalar.activation(out=f1w[c][:, t, :], in_=raw.bitcast(FP8), func=ACT.Copy, scale=f1s[:, t : t + 1])
-            else:
-                nc.vector.tensor_scalar(out=f1w[c][:, t, :], in0=raw.bitcast(FP8), scalar1=f1s[:, t : t + 1], scalar2=None, op0=ALU.mult)
-
-        def interleave(dst, src, h, n):
+        def interleave(mixed, planes, h):
+            cols = slice(HALF * h, HALF * (h + 1))
             nc.vector.tensor_copy(
-                out=dst[:, n * h : n * (h + 1), :].rearrange("p (b i) t -> p b t i", i=4),
-                in_=src[:, :, n * h : n * (h + 1)].rearrange("p t (b i) -> p b t i", i=4),
+                out=mixed[:, cols, :].rearrange("p (b i) t -> p b t i", i=4),
+                in_=planes[:, :, cols].rearrange("p t (b i) -> p b t i", i=4),
             )
 
-        def quant(codes, scales, src, h, n):
+        def quantise(operand, mixed, n0, n1):
+            codes, scales = operand
             nc.vector.quantize_mx(
-                out=codes[:, n * h : n * (h + 1)].bitcast(FP8X4),
-                scales=scales[:, n * h : n * (h + 1)],
-                in_=src[:, n * h : n * (h + 1), :].rearrange("p n t -> p (n t)"),
+                out=codes[:, n0:n1].bitcast(FP8X4),
+                scales=scales[:, n0:n1],
+                in_=mixed[:, n0:n1, :].rearrange("p n t -> p (n t)"),
             )
 
-        def f1_inter(c, h, n=256):
-            if c not in f1i:
-                f1i[c] = work.tile([P, 512, 4], BF16, name="f1i", align_bytes=64)
-            interleave(f1i[c], f1w[c], h, n)
+        def operand_tiles(name):
+            codes = keep.tile([P, N], U32, name=name + "_codes", align_bytes=64)
+            scales = keep.tile([P, N], U8, name=name + "_scales", align_bytes=64)
+            return codes, scales
 
-        def f1_quant(c, h, n=256):
-            if c not in f1c:
-                f1c[c] = keep.tile([P, 512], U32, name=f"f1c{c}", align_bytes=64)
-                f1p[c] = keep.tile([P, 512], U8, name=f"f1p{c}", align_bytes=64)
-            quant(f1c[c], f1p[c], f1i[c], h, n)
+        f1_planes, f1_mixed, f1_mx = {}, {}, {}
 
-        f2i, f2c, f2p = {}, {}, {}
+        def f1_widen(c, k, on_scalar):
+            if c not in f1_planes:
+                f1_planes[c] = work.tile([P, PACK, N], BF16, name="f1_planes")
+            raw = (f1_raw0[:, k, :], f1_raw1[:, k, :], f1_raw23[:, k, 0:N], f1_raw23[:, k, N : 2 * N])[c]
+            plane = f1_planes[c][:, k, :]
+            factor = f1_factor[:, k : k + 1]
+            if on_scalar:
+                nc.scalar.activation(out=plane, in_=raw.bitcast(FP8), func=ACT.Copy, scale=factor)
+            else:
+                nc.vector.tensor_scalar(
+                    out=plane, in0=raw.bitcast(FP8), scalar1=factor, scalar2=None, op0=ALU.mult
+                )
 
-        def f2_inter(g, h, eng):
-            if g not in f2i:
-                f2i[g] = work.tile([P, 512, 4], BF16, name="f2i", align_bytes=64)
-            dst = f2i[g][:, 256 * h : 256 * (h + 1), :].rearrange("p (j m) c -> p m c j", j=2)
-            src = f2r[g][:].rearrange("p c (m j) -> p m c j", j=4)[:, :, :, 2 * h : 2 * h + 2]
-            if eng == "s":
+        def f1_interleave(c):
+            f1_mixed[c] = work.tile([P, N, PACK], BF16, name="f1_mixed", align_bytes=64)
+            for h in range(2):
+                interleave(f1_mixed[c], f1_planes[c], h)
+
+        def f1_quantise(c, step):
+            f1_mx[c] = operand_tiles(f"f1_{c}")
+            for n in range(0, N, step):
+                quantise(f1_mx[c], f1_mixed[c], n, n + step)
+
+        f2_mixed, f2_mx = {}, {}
+
+        def f2_interleave(g, h, on_scalar):
+            if g not in f2_mixed:
+                f2_mixed[g] = work.tile([P, N, PACK], BF16, name="f2_mixed", align_bytes=64)
+            dst = f2_mixed[g][:, HALF * h : HALF * (h + 1), :].rearrange("p (j m) c -> p m c j", j=2)
+            src = f2_raw[g][:].rearrange("p c (m j) -> p m c j", j=PACK)[:, :, :, 2 * h : 2 * h + 2]
+            if on_scalar:
                 nc.scalar.copy(out=dst, in_=src)
             else:
                 nc.vector.tensor_copy(out=dst, in_=src)
 
-        def f2_quant(g, h):
-            if g not in f2c:
-                f2c[g] = keep.tile([P, 512], U32, name=f"f2c{g}", align_bytes=64)
-                f2p[g] = keep.tile([P, 512], U8, name=f"f2p{g}", align_bytes=64)
-            quant(f2c[g], f2p[g], f2i[g], h, 256)
+        def f2_quantise(g, step):
+            f2_mx[g] = operand_tiles(f"f2_{g}")
+            for n in range(0, N, step):
+                quantise(f2_mx[g], f2_mixed[g], n, n + step)
 
-        hp, hi, hc, hs = {}, {}, {}, {}
+        h_planes, h_mixed, h_mx = {}, {}, {}
 
-        corr = {}
-
-        def a_mm(u, j, n0=0, n1=512):
-            c, g = divmod(u, G)
-            ps = ring.tile([P, n1 - n0], F32, name="corr")
-            corr[u, j] = ps
+        def correlate(u, j, n0, n1):
+            c, g = divmod(u, GROUPS)
+            if u not in h_planes:
+                h_planes[u] = work.tile([P, PACK, N], BF16, name="h_planes")
+            (f2_codes, f2_scales), (f1_codes, f1_scales) = f2_mx[g], f1_mx[c]
+            bank = ring.tile([P, n1 - n0], F32, name="bank")
             nc.tensor.matmul_mx(
-                out=ps[:],
-                lhsT=f2c[g][:, 128 * j : 128 * (j + 1)].bitcast(FP8X4),
-                lhsT_scale=f2p[g][:, 128 * j : 128 * (j + 1)],
-                rhs=f1c[c][:, n0:n1].bitcast(FP8X4),
-                rhs_scale=f1p[c][:, n0:n1],
+                out=bank[:],
+                lhsT=f2_codes[:, P * j : P * (j + 1)].bitcast(FP8X4),
+                lhsT_scale=f2_scales[:, P * j : P * (j + 1)],
+                rhs=f1_codes[:, n0:n1].bitcast(FP8X4),
+                rhs_scale=f1_scales[:, n0:n1],
                 start=True,
                 stop=True,
             )
-
-        def a_act(u, j, n0=0, n1=512):
-            c, g = divmod(u, G)
-            if u not in hp:
-                hp[u] = work.tile([P, 4, 512], BF16, name="hp")
-            nc.scalar.activation(out=hp[u][:, j, n0:n1], in_=corr[u, j][:], func=ACT.Relu, bias=bias_t[:, g, j : j + 1])
-
-        def h_inter(u, h, n=256):
-            if u not in hi:
-                hi[u] = work.tile([P, 512, 4], BF16, name="hi", align_bytes=64)
-            interleave(hi[u], hp[u], h, n)
-
-        def h_quant(u, h, n=256):
-            if u not in hc:
-                hc[u] = keep.tile([P, 512], U32, name=f"hc{u}", align_bytes=64)
-                hs[u] = keep.tile([P, 512], U8, name=f"hs{u}", align_bytes=64)
-            quant(hc[u], hs[u], hi[u], h, n)
-
-        def bias_grid(g):
-            return bias_t[:, g, :].unsqueeze(1).to_broadcast([P, 128, 4])
-
-        def v_mm(u, n):
-            c, g = divmod(u, G)
-            ps = ring.tile([P, 4, 128], F32, name="corr")
-            corr[u, "v", n] = ps
-            for j in range(4):
-                nc.tensor.matmul_mx(
-                    out=ps[:, j, :],
-                    lhsT=f2c[g][:, 128 * j : 128 * (j + 1)].bitcast(FP8X4),
-                    lhsT_scale=f2p[g][:, 128 * j : 128 * (j + 1)],
-                    rhs=f1c[c][:, 128 * n : 128 * (n + 1)].bitcast(FP8X4),
-                    rhs_scale=f1p[c][:, 128 * n : 128 * (n + 1)],
-                    start=True,
-                    stop=True,
-                )
-
-        def v_add(u, n):
-            g = u % G
-            if u not in hi:
-                hi[u] = work.tile([P, 512, 4], BF16, name="hi", align_bytes=64)
-            nc.vector.tensor_tensor(
-                out=hi[u][:, 128 * n : 128 * (n + 1), :],
-                in0=corr[u, "v", n][:].rearrange("p j n -> p n j"),
-                in1=bias_grid(g),
-                op=ALU.add,
+            nc.scalar.activation(
+                out=h_planes[u][:, j, n0:n1], in_=bank[:], func=ACT.Relu, bias=bias_t[:, g, j : j + 1]
             )
 
-        def v_relu(u, h):
-            flat = hi[u][:, 256 * h : 256 * (h + 1), :].rearrange("p n t -> p (n t)")
-            nc.vector.tensor_scalar(out=flat, in0=flat, scalar1=0.0, scalar2=None, op0=ALU.max)
+        def h_interleave(u, h):
+            if u not in h_mixed:
+                h_mixed[u] = work.tile([P, N, PACK], BF16, name="h_mixed", align_bytes=64)
+            interleave(h_mixed[u], h_planes[u], h)
 
-        ybig, ysml, osb = {}, {}, {}
+        def h_quantise(u, h):
+            if u not in h_mx:
+                h_mx[u] = operand_tiles(f"h_{u}")
+            quantise(h_mx[u], h_mixed[u], HALF * h, HALF * (h + 1))
 
-        def b_mm(u, k, ps, n0, n1, start, stop):
-            g = u % G
+        fine, coarse, result = {}, {}, {}
+
+        def pool_pass(u, k, psum, n0, n1):
+            g = u % GROUPS
+            h_codes, h_scales = h_mx[u]
             nc.tensor.matmul_mx(
-                out=ps,
-                lhsT=hc[u][:, 128 * k : 128 * (k + 1)].bitcast(FP8X4),
-                lhsT_scale=hs[u][:, 128 * k : 128 * (k + 1)],
-                rhs=ww[:, g, 2 * n0 : 2 * n1].bitcast(FP4X4),
-                rhs_scale=ws[:, g, n0:n1],
-                start=start,
-                stop=stop,
+                out=psum,
+                lhsT=h_codes[:, P * k : P * (k + 1)].bitcast(FP8X4),
+                lhsT_scale=h_scales[:, P * k : P * (k + 1)],
+                rhs=words[:, g, 2 * n0 : 2 * n1].bitcast(FP4X4),
+                rhs_scale=w_scales[:, g, n0:n1],
+                start=(g == 0),
+                stop=(g == GROUPS - 1),
             )
 
-        def b_big(u, k):
-            c, g = divmod(u, G)
+        def pool_fine(u, k):
+            c, g = divmod(u, GROUPS)
             if g == 0:
-                ybig[c, k] = ypool.tile([P, 512], F32, name=f"y{k}")
-            b_mm(u, k, ybig[c, k][:], 0, 512, g == 0, g == G - 1)
+                fine[c, k] = sums.tile([P, FINE], F32, name=f"fine{k}")
+            pool_pass(u, k, fine[c, k][:], 0, FINE)
 
-        def b_sml(c, k, g):
-            if c not in ysml:
-                ysml[c] = ypool.tile([P, 4, 128], F32, name="ys")
-            b_mm(c * G + g, k, ysml[c][:, k, :], 512, 640, g == 0, g == G - 1)
+        def pool_coarse(c, k):
+            if c not in coarse:
+                coarse[c] = sums.tile([P, TILES, C - FINE], F32, name="coarse")
+            for g in range(GROUPS):
+                pool_pass(GROUPS * c + g, k, coarse[c][:, k, :], FINE, C)
 
-        def o_tile(c, k):
-            if c not in osb:
-                osb[c] = work.tile([P, 4, C], F32, name="osb", bufs=2)
-            return osb[c][:, k, :]
-
-        def y_out(c, k, eng, ps, n0, n1):
-            o = o_tile(c, k)
-            cf = conf_t[:, 4 * c + k : 4 * c + k + 1]
-            if eng == "s":
-                nc.scalar.activation(out=o[:, n0:n1], in_=ps, func=ACT.Copy, scale=cf)
+        def take_out(c, k, psum, n0, n1, on_scalar):
+            if c not in result:
+                result[c] = work.tile([P, TILES, C], F32, name="result", bufs=2)
+            dst = result[c][:, k, n0:n1]
+            factor = conf_t[:, TILES * c + k : TILES * c + k + 1]
+            if on_scalar:
+                nc.scalar.activation(out=dst, in_=psum, func=ACT.Copy, scale=factor)
             else:
-                nc.vector.tensor_scalar(out=o[:, n0:n1], in0=ps, scalar1=cf, scalar2=None, op0=ALU.mult)
+                nc.vector.tensor_scalar(out=dst, in0=psum, scalar1=factor, scalar2=None, op0=ALU.mult)
 
-        def y_small(c):
-            o_tile(c, 0)
+        def take_coarse(c, psum, tiles):
             nc.vector.tensor_tensor(
-                out=osb[c][:, :, 512:640],
-                in0=ysml[c][:],
-                in1=conf_t[:, 4 * c : 4 * c + 4].unsqueeze(2).to_broadcast([P, 4, 128]),
+                out=result[c][:, 0:tiles, FINE:C],
+                in0=psum,
+                in1=conf_t[:, TILES * c : TILES * c + tiles].unsqueeze(2).to_broadcast([P, tiles, C - FINE]),
                 op=ALU.mult,
             )
 
-        def store(c, k):
-            r0 = 512 * c + 128 * k
-            nc.sync.dma_start(out=out[r0 : r0 + 128, :], in_=osb[c][:, k, :])
+        def store(c, k, n0, n1):
+            s0 = N * c + P * k
+            nc.sync.dma_start(out=out[s0 : s0 + P, n0:n1], in_=result[c][:, k, n0:n1])
 
-        S_AT, V_AT = {}, {}
-
-        def at(eng, pos, fn, *args):
-            (S_AT if eng == "s" else V_AT).setdefault(pos, []).append((fn, args))
-
-        for g in range(G):
-            for h in range(2):
-                e, pos = CFG["p"][2 * g + h]
-                at(e, pos, f2_inter, g, h, e)
-            if CFG["pq"][g] is not None:
-                at("v", CFG["pq"][g], f2_quant, g, 0)
-                at("v", CFG["pq"][g], f2_quant, g, 1)
-        for c in range(4):
-            for t in range(4):
-                e, pos = CFG["w"][4 * c + t]
-                at(e, pos, f1_widen, c, e, t)
-            for h in range(2):
-                at("v", CFG["fi"][c], f1_inter, c, h)
-            for h in range(2):
-                at("v", CFG["fq"][c], f1_quant, c, h)
-
-        def ybig_out(c, k, e):
-            y_out(c, k, e, ybig[c, k][:], 0, 512)
-
-        def small_out(c, e):
-            if e == "v":
-                y_small(c)
+        def finish(c, on_scalar):
+            if on_scalar:
+                for k in range(TILES):
+                    take_out(c, k, coarse[c][:, k, :], FINE, C, True)
             else:
-                for k in range(4):
-                    y_out(c, k, "s", ysml[c][:, k, :], 512, 640)
-            for k in range(4):
-                store(c, k)
+                take_coarse(c, coarse[c][:], TILES)
+            for k in range(TILES):
+                store(c, k, 0, C)
 
-        for c in range(3):
-            for k in range(4):
-                e, pos = CFG["y"][4 * c + k]
-                at(e, pos, ybig_out, c, k, e)
-            e, pos = CFG["ys"][c]
-            at(e, pos, small_out, c, e)
+        def before_slot(slot):
+            if slot in WIDEN_2_SLOTS:
+                f1_widen(2, WIDEN_2_SLOTS.index(slot), True)
+            if slot == WIDEN_3_SLOT:
+                f1_widen(3, 0, True)
+            for c in range(CHUNKS - 1):
+                k, odd = divmod(slot - SUM_SLOT[c], 2)
+                if odd == 0 and 0 <= k < SUM_TILES[c]:
+                    take_out(c, k, fine[c, k][:], 0, FINE, True)
+            if slot == 62:
+                finish(2, True)
 
-        def go(d, pos):
-            for fn, args in d.get(pos, ()):
-                fn(*args)
-
-        tp = ypool.tile([P, P], BF16, name="ys")
-        conf_t = keep.tile([P, 16], F32, name="conf_t")
-        for i in range(-9, 0):
-            go(S_AT, i)
-            go(V_AT, i)
-        LAG = CFG["lag"]
-        VU = CFG["vu"]
-        HALF = CFG["half"]
-        for u in range(16 + LAG):
-            v = u - LAG
-            cv, gv = divmod(v, G)
-            first = v >= G and gv == 0
-            second = v >= G and gv == 1
-            for j in range(4):
-                go(S_AT, 4 * u + j)
-                if u < 16:
-                    if u in VU:
-                        v_mm(u, j)
-                    elif u in HALF:
-                        a_mm(u, j, 0, 256)
-                        a_act(u, j, 0, 256)
-                    else:
-                        a_mm(u, j)
-                        a_act(u, j)
-                if first:
-                    for g in range(G):
-                        b_sml(cv - 1, j, g)
-                    if j >= CFG["bj"]:
-                        b_big(v, j - CFG["bj"])
-                elif second:
-                    for i in CFG["sec"][j]:
-                        b_big(v - 1 if i < 4 else v, i % 4)
-                elif 0 <= v < 15:
-                    b_big(v, j)
+        def before_unit(u):
             if u == 2:
-                nc.tensor.transpose(tp[:], cz[:], ident[:])
-                nc.scalar.copy(out=conf_t[:], in_=tp[:, 0:16])
-            if u in CFG["tv"]:
-                v_mm(u, 2)
-                v_mm(u, 3)
-            elif u in HALF:
-                for j in range(4):
-                    a_mm(u, j, 256, 512)
-                    a_act(u, j, 256, 512)
-            go(V_AT, 2 * u)
-            if u in VU:
-                v_add(u, 0)
-                v_add(u, 1)
-                v_add(u, 2)
-                v_relu(u, 0)
-                v_add(u, 3)
-                h_quant(u, 0)
-                v_relu(u, 1)
-                go(V_AT, 2 * u + 1)
-                h_quant(u, 1)
-            elif u in CFG["tv"]:
-                v_add(u, 2)
-                v_add(u, 3)
-                v_relu(u, 1)
-                h_inter(u, 0)
-                h_quant(u, 1)
-                go(V_AT, 2 * u + 1)
-                h_quant(u, 0)
-            elif u < 16:
-                h_inter(u, 0)
-                if u in HALF:
-                    h_quant(u, 0)
-                    h_inter(u, 1)
-                    go(V_AT, 2 * u + 1)
-                    h_quant(u, 1)
-                else:
-                    h_inter(u, 1)
-                    go(V_AT, 2 * u + 1)
-                    h_quant(u, 0)
-                    h_quant(u, 1)
+                f2_quantise(3, N)
+                f1_interleave(1)
+            if u == 4:
+                f1_interleave(2)
+            if u == 6:
+                for k in range(1, PACK):
+                    f1_widen(3, k, False)
+            if u == 8:
+                f1_interleave(3)
+            if u == 10:
+                f1_quantise(3, N)
+            for c in range(CHUNKS - 1):
+                if u == GROUPS * (c + 1) + LAG:
+                    for k in range(SUM_TILES[c], TILES):
+                        take_out(c, k, fine[c, k][:], 0, FINE, False)
+            if u == 7:
+                finish(0, False)
+            if u == 12:
+                finish(1, False)
+
+        def inside_unit(u):
+            if u == 2:
+                f1_quantise(1, N)
+            if u == 5:
+                f1_quantise(2, N)
+
+        for k in range(PACK):
+            f1_widen(0, k, k == 2)
+        f1_interleave(0)
+        f1_quantise(0, HALF)
+        f2_interleave(0, 0, False)
+        f2_interleave(1, 1, False)
+        f2_interleave(0, 1, True)
+        f2_quantise(0, HALF)
+        f2_interleave(1, 0, False)
+        f2_interleave(2, 0, False)
+        f2_interleave(3, 0, False)
+        for k in range(PACK):
+            f1_widen(1, k, True)
+        f2_interleave(2, 1, True)
+        f2_quantise(1, N)
+        f2_quantise(2, N)
+        f2_interleave(3, 1, False)
+
+        last = UNITS - 1
+        for u in range(UNITS):
+            v = u - LAG
+            first, second = v >= GROUPS and v % GROUPS == 0, v >= GROUPS and v % GROUPS == 1
+            for j in range(PACK):
+                before_slot(PACK * u + j)
+                correlate(u, j, 0, HALF if u == last else N)
+                if first:
+                    pool_coarse(v // GROUPS - 1, j)
+                elif second:
+                    pool_fine(v - 1, j)
+                    pool_fine(v, j)
+                elif v >= 0:
+                    pool_fine(v, j)
+            if u == 2:
+                turned = sums.tile([P, P], BF16, name="coarse")
+                nc.tensor.transpose(turned[:], conf_rows[:], ident[:])
+                nc.scalar.copy(out=conf_t[:], in_=turned[:, 0 : S // P])
+            if u == last:
+                for j in range(PACK):
+                    correlate(u, j, HALF, N)
+                    if j:
+                        for k in range(j - 1, TILES if j == PACK - 1 else j):
+                            pool_fine(u - 1, k)
+            before_unit(u)
+            if u == last:
+                for h in range(2):
+                    h_interleave(u, h)
+                    h_quantise(u, h)
             else:
-                go(V_AT, 2 * u + 1)
-        sm = [ypool.tile([P, 128], F32, name="ys")]
-        for k in range(1, 4):
-            t = ring.tile([P, 128], F32, name="corr")
-            sm.append(t)
-        for g in range(3):
-            for k in range(4):
-                b_mm(12 + g, k, sm[k][:], 512, 640, g == 0, False)
-        for k in range(4):
-            b_big(15, k)
-            b_mm(15, k, sm[k][:], 512, 640, False, True)
-            e1, e2 = CFG["end"][k]
-            y_out(3, k, e1, ybig[3, k][:], 0, 512)
-            y_out(3, k, e2, sm[k][:], 512, 640)
-            r0 = 1536 + 128 * k
-            nc.sync.dma_start(out=out[r0 : r0 + 128, 0:512], in_=osb[3][:, k, 0:512])
-            nc.sync.dma_start(out=out[r0 : r0 + 128, 512:640], in_=osb[3][:, k, 512:640])
+                for h in range(2):
+                    h_interleave(u, h)
+                inside_unit(u)
+                for h in range(2):
+                    h_quantise(u, h)
+
+        c = CHUNKS - 1
+        pair = sums.tile([P, 2, C - FINE], F32, name="coarse")
+        single = {}
+        for k in (2, 3):
+            single[k] = ring.tile([P, C - FINE], F32, name="bank")
+
+        def last_fine(k, on_scalar):
+            pool_fine(last, k)
+            take_out(c, k, fine[c, k][:], 0, FINE, on_scalar)
+            store(c, k, 0, FINE)
+
+        last_fine(0, True)
+        last_fine(1, True)
+        for g in range(GROUPS - 1):
+            for k in (2, 3):
+                pool_pass(GROUPS * c + g, k, single[k][:], FINE, C)
+        last_fine(2, False)
+        last_fine(3, True)
+        for k in (2, 3):
+            pool_pass(last, k, single[k][:], FINE, C)
+            take_out(c, k, single[k][:], FINE, C, k == 2)
+            store(c, k, FINE, C)
+        for k in (0, 1):
+            for g in range(GROUPS):
+                pool_pass(GROUPS * c + g, k, pair[:, k, :], FINE, C)
+        take_coarse(c, pair[:], 2)
+        nc.sync.dma_start(
+            out=out[N * c : N * c + 2 * P, FINE:C].rearrange("(k p) n -> p k n", p=P),
+            in_=result[c][:, 0:2, FINE:C],
+        )

from contextlib import ExitStack

import concourse.mybir as mybir
from concourse.masks import make_identity

D, S, T, C = 512, 2048, 2048, 640
FLOPS = 2 * D * S * T + 2 * S * T * C

F32 = mybir.dt.float32
BF16 = mybir.dt.bfloat16
U32 = mybir.dt.uint32
I32 = mybir.dt.int32
U8 = mybir.dt.uint8
FP8 = mybir.dt.float8_e4m3fn
FP8X4 = mybir.dt.float8_e4m3fn_x4
FP4X4 = mybir.dt.float4_e2m1fn_x4
ACT = mybir.ActivationFunctionType
ALU = mybir.AluOpType

P = 128
PACK = 4
N = 512
HALF = N // 2
GROUPS = T // N
CHUNKS = S // N
UNITS = GROUPS * CHUNKS
TILES = N // P
FINE = 512
LAG = 2

WIDEN_2_SLOTS = (10, 12, 14, 16)
WIDEN_3_SLOT = 26
SUM_SLOT = (24, 40, 57)
SUM_TILES = (3, 3, 2)


def tile_raft_pyramid_pooling_s13_kernel(
    tc, f1_bytes, f1_scale, f2, bias, pool_words, pool_scales, conf, out
):
    nc = tc.nc
    with ExitStack() as ctx:
        keep = ctx.enter_context(tc.tile_pool(name="keep", bufs=1))
        work = ctx.enter_context(tc.tile_pool(name="work", bufs=3))
        ring = ctx.enter_context(tc.psum_pool(name="ring", bufs=3))
        sums = ctx.enter_context(tc.psum_pool(name="sums", bufs=1))
        ctx.enter_context(tc.manual_schedule())

        f1_factor = keep.tile([P, PACK], F32, name="f1_factor")
        nc.scalar.dma_start(out=f1_factor[:], in_=f1_scale.rearrange("(p c) o -> p (c o)", c=PACK))
        bias_bf = keep.tile([P, GROUPS, PACK], BF16, name="bias_bf")
        nc.scalar.dma_start(out=bias_bf[:], in_=bias.rearrange("(g p j) -> p g j", p=P, j=PACK))

        f1_rows = f1_bytes.rearrange("(p c) s -> p c s", c=PACK)
        f2_rows = f2.rearrange("(p c) t -> p c t", c=PACK)

        def load_f1(name, s0, s1):
            bytes_in = keep.tile([P, PACK, s1 - s0], U8, name=name)
            nc.sync.dma_start(out=bytes_in[:], in_=f1_rows[:, :, s0:s1])
            return bytes_in

        def load_f2(g):
            rows = keep.tile([P, PACK, N], BF16, name=f"f2_raw{g}")
            nc.sync.dma_start(out=rows[:], in_=f2_rows[:, :, N * g : N * (g + 1)])
            return rows

        f1_raw0 = load_f1("f1_raw0", 0, N)
        f2_raw = [load_f2(0)]
        f1_raw1 = load_f1("f1_raw1", N, 2 * N)
        for g in range(1, GROUPS):
            f2_raw.append(load_f2(g))
        words = keep.tile([P, GROUPS, 2 * C], U8, name="words", align_bytes=64)
        nc.sync.dma_start(out=words[:], in_=pool_words.rearrange("g p b -> p g b"))
        w_scales = keep.tile([P, GROUPS, C], U8, name="w_scales", align_bytes=64)
        w_scales_i32 = w_scales[:].rearrange("p g n -> p (g n)").bitcast(I32)
        nc.vector.memset(w_scales_i32, 0)
        for q in range(4):
            nc.sync.dma_start(
                out=w_scales_i32[32 * q : 32 * q + 4, :].rearrange("p (g n) -> p g n", g=GROUPS),
                in_=pool_scales.bitcast(I32)[:, 4 * q : 4 * q + 4, :].rearrange("g r n -> r g n"),
            )
        f1_raw23 = load_f1("f1_raw23", 2 * N, 4 * N)

        ident = keep.tile([P, P], BF16, name="ident")
        make_identity(nc, ident[:])
        bias_t = keep.tile([P, GROUPS, PACK], F32, name="bias_t")
        nc.gpsimd.tensor_copy(out=bias_t[:], in_=bias_bf[:])
        conf_rows = keep.tile([P, P], BF16, name="conf_rows")
        nc.gpsimd.memset(conf_rows[:], 0.0)
        nc.sync.dma_start(out=conf_rows[0 : S // P, :], in_=conf.rearrange("(i p) -> i p", p=P))
        conf_t = keep.tile([P, S // P], F32, name="conf_t")
        dummy = keep.tile([P, 1], F32, name="dummy")
        nc.vector.memset(dummy[:], 0.0)
        nc.scalar.activation(out=dummy[:], in_=dummy[:], func=ACT.Relu)

        def interleave(mixed, planes, h):
            cols = slice(HALF * h, HALF * (h + 1))
            nc.vector.tensor_copy(
                out=mixed[:, cols, :].rearrange("p (b i) t -> p b t i", i=4),
                in_=planes[:, :, cols].rearrange("p t (b i) -> p b t i", i=4),
            )

        def quantise(operand, mixed, n0, n1):
            codes, scales = operand
            nc.vector.quantize_mx(
                out=codes[:, n0:n1].bitcast(FP8X4),
                scales=scales[:, n0:n1],
                in_=mixed[:, n0:n1, :].rearrange("p n t -> p (n t)"),
            )

        def operand_tiles(name):
            codes = keep.tile([P, N], U32, name=name + "_codes", align_bytes=64)
            scales = keep.tile([P, N], U8, name=name + "_scales", align_bytes=64)
            return codes, scales

        f1_planes, f1_mixed, f1_mx = {}, {}, {}

        def f1_widen(c, k, on_scalar):
            if c not in f1_planes:
                f1_planes[c] = work.tile([P, PACK, N], BF16, name="f1_planes")
            raw = (f1_raw0[:, k, :], f1_raw1[:, k, :], f1_raw23[:, k, 0:N], f1_raw23[:, k, N : 2 * N])[c]
            plane = f1_planes[c][:, k, :]
            factor = f1_factor[:, k : k + 1]
            if on_scalar:
                nc.scalar.activation(out=plane, in_=raw.bitcast(FP8), func=ACT.Copy, scale=factor)
            else:
                nc.vector.tensor_scalar(
                    out=plane, in0=raw.bitcast(FP8), scalar1=factor, scalar2=None, op0=ALU.mult
                )

        def f1_interleave(c):
            f1_mixed[c] = work.tile([P, N, PACK], BF16, name="f1_mixed", align_bytes=64)
            for h in range(2):
                interleave(f1_mixed[c], f1_planes[c], h)

        def f1_quantise(c, step):
            f1_mx[c] = operand_tiles(f"f1_{c}")
            for n in range(0, N, step):
                quantise(f1_mx[c], f1_mixed[c], n, n + step)

        f2_mixed, f2_mx = {}, {}

        def f2_interleave(g, h, on_scalar):
            if g not in f2_mixed:
                f2_mixed[g] = work.tile([P, N, PACK], BF16, name="f2_mixed", align_bytes=64)
            dst = f2_mixed[g][:, HALF * h : HALF * (h + 1), :].rearrange("p (j m) c -> p m c j", j=2)
            src = f2_raw[g][:].rearrange("p c (m j) -> p m c j", j=PACK)[:, :, :, 2 * h : 2 * h + 2]
            if on_scalar:
                nc.scalar.copy(out=dst, in_=src)
            else:
                nc.vector.tensor_copy(out=dst, in_=src)

        def f2_quantise(g, step):
            f2_mx[g] = operand_tiles(f"f2_{g}")
            for n in range(0, N, step):
                quantise(f2_mx[g], f2_mixed[g], n, n + step)

        h_planes, h_mixed, h_mx = {}, {}, {}

        def correlate(u, j, n0, n1):
            c, g = divmod(u, GROUPS)
            if u not in h_planes:
                h_planes[u] = work.tile([P, PACK, N], BF16, name="h_planes")
            (f2_codes, f2_scales), (f1_codes, f1_scales) = f2_mx[g], f1_mx[c]
            bank = ring.tile([P, n1 - n0], F32, name="bank")
            nc.tensor.matmul_mx(
                out=bank[:],
                lhsT=f2_codes[:, P * j : P * (j + 1)].bitcast(FP8X4),
                lhsT_scale=f2_scales[:, P * j : P * (j + 1)],
                rhs=f1_codes[:, n0:n1].bitcast(FP8X4),
                rhs_scale=f1_scales[:, n0:n1],
                start=True,
                stop=True,
            )
            nc.scalar.activation(
                out=h_planes[u][:, j, n0:n1], in_=bank[:], func=ACT.Relu, bias=bias_t[:, g, j : j + 1]
            )

        def h_interleave(u, h):
            if u not in h_mixed:
                h_mixed[u] = work.tile([P, N, PACK], BF16, name="h_mixed", align_bytes=64)
            interleave(h_mixed[u], h_planes[u], h)

        def h_quantise(u, h):
            if u not in h_mx:
                h_mx[u] = operand_tiles(f"h_{u}")
            quantise(h_mx[u], h_mixed[u], HALF * h, HALF * (h + 1))

        fine, coarse, result = {}, {}, {}

        def pool_pass(u, k, psum, n0, n1):
            g = u % GROUPS
            h_codes, h_scales = h_mx[u]
            nc.tensor.matmul_mx(
                out=psum,
                lhsT=h_codes[:, P * k : P * (k + 1)].bitcast(FP8X4),
                lhsT_scale=h_scales[:, P * k : P * (k + 1)],
                rhs=words[:, g, 2 * n0 : 2 * n1].bitcast(FP4X4),
                rhs_scale=w_scales[:, g, n0:n1],
                start=(g == 0),
                stop=(g == GROUPS - 1),
            )

        def pool_fine(u, k):
            c, g = divmod(u, GROUPS)
            if g == 0:
                fine[c, k] = sums.tile([P, FINE], F32, name=f"fine{k}")
            pool_pass(u, k, fine[c, k][:], 0, FINE)

        def pool_coarse(c, k):
            if c not in coarse:
                coarse[c] = sums.tile([P, TILES, C - FINE], F32, name="coarse")
            for g in range(GROUPS):
                pool_pass(GROUPS * c + g, k, coarse[c][:, k, :], FINE, C)

        def take_out(c, k, psum, n0, n1, on_scalar):
            if c not in result:
                result[c] = work.tile([P, TILES, C], F32, name="result", bufs=2)
            dst = result[c][:, k, n0:n1]
            factor = conf_t[:, TILES * c + k : TILES * c + k + 1]
            if on_scalar:
                nc.scalar.activation(out=dst, in_=psum, func=ACT.Copy, scale=factor)
            else:
                nc.vector.tensor_scalar(out=dst, in0=psum, scalar1=factor, scalar2=None, op0=ALU.mult)

        def take_coarse(c, psum, tiles):
            nc.vector.tensor_tensor(
                out=result[c][:, 0:tiles, FINE:C],
                in0=psum,
                in1=conf_t[:, TILES * c : TILES * c + tiles].unsqueeze(2).to_broadcast([P, tiles, C - FINE]),
                op=ALU.mult,
            )

        def store(c, k, n0, n1):
            s0 = N * c + P * k
            nc.sync.dma_start(out=out[s0 : s0 + P, n0:n1], in_=result[c][:, k, n0:n1])

        def finish(c, on_scalar):
            if on_scalar:
                for k in range(TILES):
                    take_out(c, k, coarse[c][:, k, :], FINE, C, True)
            else:
                take_coarse(c, coarse[c][:], TILES)
            for k in range(TILES):
                store(c, k, 0, C)

        def before_slot(slot):
            if slot in WIDEN_2_SLOTS:
                f1_widen(2, WIDEN_2_SLOTS.index(slot), True)
            if slot == WIDEN_3_SLOT:
                f1_widen(3, 0, True)
            for c in range(CHUNKS - 1):
                k, odd = divmod(slot - SUM_SLOT[c], 2)
                if odd == 0 and 0 <= k < SUM_TILES[c]:
                    take_out(c, k, fine[c, k][:], 0, FINE, True)
            if slot == 62:
                finish(2, True)

        def before_unit(u):
            if u == 2:
                f2_quantise(3, N)
                f1_interleave(1)
            if u == 4:
                f1_interleave(2)
            if u == 6:
                for k in range(1, PACK):
                    f1_widen(3, k, False)
            if u == 8:
                f1_interleave(3)
            if u == 10:
                f1_quantise(3, N)
            for c in range(CHUNKS - 1):
                if u == GROUPS * (c + 1) + LAG:
                    for k in range(SUM_TILES[c], TILES):
                        take_out(c, k, fine[c, k][:], 0, FINE, False)
            if u == 7:
                finish(0, False)
            if u == 12:
                finish(1, False)

        def inside_unit(u):
            if u == 2:
                f1_quantise(1, N)
            if u == 5:
                f1_quantise(2, N)

        for k in range(PACK):
            f1_widen(0, k, k == 2)
        f1_interleave(0)
        f1_quantise(0, HALF)
        f2_interleave(0, 0, False)
        f2_interleave(1, 1, False)
        f2_interleave(0, 1, True)
        f2_quantise(0, HALF)
        f2_interleave(1, 0, False)
        f2_interleave(2, 0, False)
        f2_interleave(3, 0, False)
        for k in range(PACK):
            f1_widen(1, k, True)
        f2_interleave(2, 1, True)
        f2_quantise(1, N)
        f2_quantise(2, N)
        f2_interleave(3, 1, False)

        last = UNITS - 1
        for u in range(UNITS):
            v = u - LAG
            first, second = v >= GROUPS and v % GROUPS == 0, v >= GROUPS and v % GROUPS == 1
            for j in range(PACK):
                before_slot(PACK * u + j)
                correlate(u, j, 0, HALF if u == last else N)
                if first:
                    pool_coarse(v // GROUPS - 1, j)
                elif second:
                    pool_fine(v - 1, j)
                    pool_fine(v, j)
                elif v >= 0:
                    pool_fine(v, j)
            if u == 2:
                turned = sums.tile([P, P], BF16, name="coarse")
                nc.tensor.transpose(turned[:], conf_rows[:], ident[:])
                nc.scalar.copy(out=conf_t[:], in_=turned[:, 0 : S // P])
            if u == last:
                for j in range(PACK):
                    correlate(u, j, HALF, N)
                    if j:
                        for k in range(j - 1, TILES if j == PACK - 1 else j):
                            pool_fine(u - 1, k)
            before_unit(u)
            if u == last:
                for h in range(2):
                    h_interleave(u, h)
                    h_quantise(u, h)
            else:
                for h in range(2):
                    h_interleave(u, h)
                inside_unit(u)
                for h in range(2):
                    h_quantise(u, h)

        c = CHUNKS - 1
        pair = sums.tile([P, 2, C - FINE], F32, name="coarse")
        single = {}
        for k in (2, 3):
            single[k] = ring.tile([P, C - FINE], F32, name="bank")

        def last_fine(k, on_scalar):
            pool_fine(last, k)
            take_out(c, k, fine[c, k][:], 0, FINE, on_scalar)
            store(c, k, 0, FINE)

        last_fine(0, True)
        last_fine(1, True)
        for g in range(GROUPS - 1):
            for k in (2, 3):
                pool_pass(GROUPS * c + g, k, single[k][:], FINE, C)
        last_fine(2, False)
        last_fine(3, True)
        for k in (2, 3):
            pool_pass(last, k, single[k][:], FINE, C)
            take_out(c, k, single[k][:], FINE, C, k == 2)
            store(c, k, FINE, C)
        for k in (0, 1):
            for g in range(GROUPS):
                pool_pass(GROUPS * c + g, k, pair[:, k, :], FINE, C)
        take_coarse(c, pair[:], 2)
        nc.sync.dma_start(
            out=out[N * c : N * c + 2 * P, FINE:C].rearrange("(k p) n -> p k n", p=P),
            in_=result[c][:, 0:2, FINE:C],
        )
